import numpy as np
import ml_dtypes


def mxq(x, axis, fmt="e4m3"):
    dtype, down = {"e4m3": (ml_dtypes.float8_e4m3fn, 7), "e5m2": (ml_dtypes.float8_e5m2, 14)}[fmt]
    v = np.moveaxis(np.asarray(x, np.float32).astype(ml_dtypes.bfloat16).astype(np.float64), axis, -1)
    blocks = v.reshape(v.shape[:-1] + (-1, 32))
    amax = np.abs(blocks).max(-1, keepdims=True)
    byte = np.maximum(np.where(amax > 0, np.frexp(amax)[1] - 1 + 127, 0) - down, 1)
    scale = np.exp2(byte - 127.0)
    codes = (blocks / scale).astype(np.float32).astype(dtype).astype(np.float64)
    return np.moveaxis((codes * scale).reshape(v.shape), -1, axis)


WIDE = False


def mx_kscale(k):
    if not WIDE:
        return np.ones(k)
    levels = np.array([10, -10, 5, -5, 0])
    if k % 512:
        return np.exp2(np.random.permutation(np.resize(levels, k // 32))).repeat(32)
    a = np.empty((k // 512, 16))
    for p in range(k // 512):
        a[p, :8] = np.random.permutation(np.resize(levels, 8))
        for g in range(8):
            far = levels[np.abs(levels - a[p, g]) >= 10]
            a[p, g + 8] = far[np.random.randint(len(far))]
    return np.exp2(a.ravel()).repeat(32)


def f64(x):
    return np.asarray(x).astype(np.float64)


def striped(idx):
    return np.tile(idx.reshape(-1, 16).T, (8, 1)).astype(np.uint16)


def unstriped(offs):
    return offs[:16].T.reshape(-1).astype(np.int64)


def striped8(idx):
    return np.concatenate([x.reshape(-1, 16).T for x in idx]).astype(np.uint16)


def runs(offs, k):
    lists = np.stack([offs[16 * r : 16 * r + 16].T.reshape(-1) for r in range(8)]).astype(np.int64)
    return lists[np.arange(k) % 512 // 64]


def pack_weight(w):
    k, n = w.shape
    w = f64(np.asarray(w, np.float32).astype(ml_dtypes.bfloat16)).reshape(k // 32, 32, n)
    amax = np.abs(w).max(1)
    byte = np.clip(np.where(amax > 0, np.frexp(amax)[1] - 1 + 127 - 7, 1), 1, 254)
    scaled = (w * np.exp2(127.0 - byte)[:, None, :]).reshape(k, n).astype(np.float32)
    words = np.ascontiguousarray(scaled.reshape(k // 512, 128, 4, n).transpose(0, 1, 3, 2)).astype(ml_dtypes.float8_e4m3fn).view(np.uint8)
    return words, np.ascontiguousarray(byte.astype(np.uint8).reshape(k // 512, 16, n))


def unpack_weight(words, scales):
    g, p, n, _ = words.shape
    vals = np.ascontiguousarray(words).view(ml_dtypes.float8_e4m3fn).astype(np.float64) * np.repeat(np.exp2(scales.astype(np.float64) - 127.0), 8, axis=1)[..., None]
    return vals.transpose(0, 1, 3, 2).reshape(g * 512, n)


def relu(v):
    return np.maximum(v, 0.0)


K, T, S, N, G, H = 512, 2048, 512, 512, 2048, 512


def setup_inputs():
    n = np.random.standard_normal
    s = mx_kscale(K)[:, None]
    u = mx_kscale(S)
    packed_xT = pack_weight(n((K, T)) * s)
    packed_dT = pack_weight(n((K, G)) / s)
    return {
        "x_words": packed_xT[0],
        "x_scales": packed_xT[1],
        "d_words": packed_dT[0],
        "d_scales": packed_dT[1],
        "gn": (np.random.uniform(0.5, 1.5, (H, 1)) * u[:, None]).astype(np.float32),
        "w1": (n((H, N)) / np.sqrt(H) / u[:, None]).astype(np.float32),
        "offs": striped(np.random.permutation(T)[:S]),
        "kidx": striped8(np.random.randint(0, G, (8, H))),
        "n1": striped8(np.stack([np.random.permutation(S) for _ in range(8)])),
        "n2": striped8(np.stack([np.random.permutation(S) for _ in range(8)])),
        "n3": striped8(np.stack([np.random.permutation(S) for _ in range(8)])),
        "n4": striped8(np.stack([np.random.permutation(S) for _ in range(8)])),
    }


def reference(x_words, x_scales, d_words, d_scales, gn, w1, offs, kidx, n1, n2, n3, n4):
    d_kidx = unpack_weight(d_words, d_scales)[np.arange(K)[:, None], runs(kidx, K)]
    xq = unpack_weight(x_words, x_scales)[:, unstriped(offs)]
    s = 0.0625 * (d_kidx.T @ xq)
    z = f64(gn) * ((s[np.arange(H)[:, None], runs(n1, H)]) * (s[np.arange(H)[:, None], runs(n2, H)]))
    h = mxq(f64(w1), 0, "e4m3").T @ mxq(z, 0, "e4m3")
    return relu(h - (h[np.arange(N)[:, None], runs(n3, N)])) + 0.5 * (relu(h[np.arange(N)[:, None], runs(n4, N)] - h))

@@ -1,0 +1,229 @@
+from contextlib import ExitStack
+
+import concourse.mybir as mybir
+
+K, T, S, N, G, H = 512, 2048, 512, 512, 2048, 512
+FLOPS = 2 * K * H * S + 2 * H * N * S
+
+F32 = mybir.dt.float32
+BF16 = mybir.dt.bfloat16
+I32 = mybir.dt.int32
+U32 = mybir.dt.uint32
+U16 = mybir.dt.uint16
+U8 = mybir.dt.uint8
+FP8X4 = mybir.dt.float8_e4m3fn_x4
+ALU = mybir.AluOpType
+ACT = mybir.ActivationFunctionType
+
+P = 128
+PACK = 4
+HALVES = [(0, 256), (256, 512)]
+Z_PIECES = [(0, 256), (256, 384), (384, 512)]
+LAST_PIECES = [(0, 256), (256, 384), (384, 512)]
+
+
+def entries(offsets, lo, hi):
+    return offsets[:, lo // 16 : hi // 16]
+
+
+def tile_picked_keyprodhinge_none_p_kernel(
+    tc, x_words, x_scales, d_words, d_scales, gn, w1, offs, kidx, n1, n2, n3, n4, out
+):
+    nc = tc.nc
+    with ExitStack() as ctx:
+        lists = ctx.enter_context(tc.tile_pool(name="lists", bufs=1))
+        keep = ctx.enter_context(tc.tile_pool(name="keep", bufs=1))
+        psum = ctx.enter_context(tc.psum_pool(name="psum", bufs=1))
+
+        d_scale_table = keep.tile([P, G], U8, align_bytes=64)
+        x_scale_table = keep.tile([P, T], U8, align_bytes=64)
+        d_plane = keep.tile([P, H], U8, align_bytes=64)
+        nc.vector.memset(x_scale_table[:].bitcast(I32), 0)
+        nc.vector.memset(d_plane[:].bitcast(I32), 0)
+
+        kidx_sb = lists.tile([P, H // 16], U16)
+        offs_sb = lists.tile([P, S // 16], U16)
+        n1_sb = lists.tile([P, S // 16], U16)
+        n2_sb = lists.tile([P, S // 16], U16)
+        n3_sb = lists.tile([P, S // 16], U16)
+        n4_sb = lists.tile([P, S // 16], U16)
+        d_word_table = keep.tile([P, G], U32, align_bytes=64)
+        x_word_table = keep.tile([P, T], U32, align_bytes=64)
+        gn_sb = keep.tile([P, PACK], F32)
+        w_raw = keep.tile([P, PACK, N], F32)
+
+        nc.sync.dma_start(kidx_sb[:], kidx)
+        nc.sync.dma_start(
+            d_scale_table[:].bitcast(I32), d_scales[0].bitcast(I32).unsqueeze(1).broadcast_to([16, 8, G // 4])
+        )
+        for q in range(4):
+            nc.scalar.dma_start(
+                x_scale_table[:].bitcast(I32)[32 * q : 32 * q + 4, :],
+                x_scales[0].bitcast(I32)[4 * q : 4 * q + 4, :],
+            )
+        nc.sync.dma_start(offs_sb[:], offs)
+        nc.sync.dma_start(
+            d_word_table[:].bitcast(I32), d_words[0].rearrange("p n t -> p (n t)").bitcast(I32)
+        )
+        nc.sync.dma_start(gn_sb[:], gn.rearrange("(p t) o -> p (t o)", t=PACK))
+        nc.sync.dma_start(
+            x_word_table[:].bitcast(I32), x_words[0].rearrange("p n t -> p (n t)").bitcast(I32)
+        )
+        nc.sync.dma_start(n1_sb[:], n1)
+        nc.sync.dma_start(n2_sb[:], n2)
+        nc.sync.dma_start(w_raw[:], w1.rearrange("(p j) n -> p j n", j=PACK))
+        nc.sync.dma_start(n3_sb[:], n3)
+        nc.sync.dma_start(n4_sb[:], n4)
+
+        gain = keep.tile([P, PACK], F32)
+        nc.scalar.activation(gain[:], gn_sb[:], ACT.Copy, scale=0.0625 * 0.0625)
+
+        d_scale_picked = keep.tile([P, H], U8, align_bytes=64)
+        nc.vector.tensor_copy(d_scale_picked[:], d_scale_table[:].indirect(kidx_sb[:]))
+        d_scale_dealt = keep.tile([P, H], U8, align_bytes=64)
+        nc.vector.tensor_copy(
+            d_scale_dealt[:].rearrange("p (t m) -> p m t", t=PACK),
+            d_scale_picked[:].rearrange("p (m t) -> p m t", t=PACK),
+        )
+        for q in range(4):
+            nc.scalar.dma_start(
+                d_plane[:].bitcast(I32)[32 * q : 32 * q + 4, :],
+                d_scale_dealt[:].bitcast(I32)[32 * q : 32 * q + 32 : 8, :],
+            )
+        x_plane = keep.tile([P, S], U8, align_bytes=64)
+        nc.vector.tensor_copy(x_plane[:], x_scale_table[:].indirect(offs_sb[:]))
+
+        d_word_picked = keep.tile([P, H], U32, align_bytes=64)
+        nc.vector.tensor_copy(d_word_picked[:], d_word_table[:].indirect(kidx_sb[:]))
+        d_codes = keep.tile([P, H], U32, align_bytes=64)
+        nc.vector.tensor_copy(
+            d_codes[:].rearrange("p (t a i) -> p a t i", t=PACK, i=4),
+            d_word_picked[:].rearrange("p (a i t) -> p a t i", t=PACK, i=4),
+        )
+
+        x_codes = keep.tile([P, S], U32, align_bytes=64)
+        s_banks = [psum.tile([P, S], F32, name="s_bank%d" % t) for t in range(PACK)]
+        for lo, hi in HALVES:
+            nc.vector.tensor_copy(x_codes[:, lo:hi], x_word_table[:].indirect(entries(offs_sb, lo, hi)))
+        for lo, hi in HALVES:
+            for t in range(PACK):
+                cols = slice(t * P, (t + 1) * P)
+                nc.tensor.matmul_mx(
+                    out=s_banks[t][:, lo:hi],
+                    lhsT=d_codes[:, cols].bitcast(FP8X4),
+                    lhsT_scale=d_plane[:, cols],
+                    rhs=x_codes[:, lo:hi].bitcast(FP8X4),
+                    rhs_scale=x_plane[:, lo:hi],
+                    start=True,
+                    stop=True,
+                )
+
+        s_plain = [keep.tile([P, S], F32, name="s_plain%d" % t) for t in range(PACK)]
+        s_gained = [keep.tile([P, S], F32, name="s_gained%d" % t) for t in range(PACK)]
+        for t in range(PACK):
+            nc.scalar.copy(s_plain[t][:], s_banks[t][:])
+        for t in range(PACK):
+            nc.scalar.activation(s_gained[t][:], s_banks[t][:], ACT.Copy, scale=gain[:, t : t + 1])
+
+        s_at_n1 = keep.tile([P, PACK, S], F32)
+        for t in range(PACK):
+            for lo, hi in HALVES:
+                nc.vector.tensor_copy(s_at_n1[:, t, lo:hi], s_plain[t][:].indirect(entries(n1_sb, lo, hi)))
+
+        w_grouped = keep.tile([P, N * PACK], BF16, align_bytes=64)
+        nc.scalar.copy(
+            w_grouped[:].rearrange("p (t m j) -> p m t j", t=PACK, j=PACK),
+            w_raw[:].rearrange("p j (m t) -> p m t j", t=PACK),
+        )
+        w_codes = keep.tile([P, N], U32, align_bytes=64)
+        w_plane = keep.tile([P, N], U8, align_bytes=64)
+
+        def quantize_w(lo, hi):
+            nc.vector.quantize_mx(
+                out=w_codes[:, lo:hi].bitcast(FP8X4), scales=w_plane[:, lo:hi], in_=w_grouped[:, PACK * lo : PACK * hi]
+            )
+
+        z_codes = keep.tile([P, S], U32, align_bytes=64)
+        z_plane = keep.tile([P, S], U8, align_bytes=64)
+        h_banks = [psum.tile([P, S], F32, name="h_bank%d" % t) for t in range(PACK)]
+        h_neg = [keep.tile([P, S], F32, name="h_neg%d" % t) for t in range(PACK)]
+        h_pos = [keep.tile([P, S], F32, name="h_pos%d" % t) for t in range(PACK)]
+
+        def second_product(t, lo, hi):
+            cols = slice(t * P, (t + 1) * P)
+            nc.tensor.matmul_mx(
+                out=h_banks[t][:, lo:hi],
+                lhsT=w_codes[:, cols].bitcast(FP8X4),
+                lhsT_scale=w_plane[:, cols],
+                rhs=z_codes[:, lo:hi].bitcast(FP8X4),
+                rhs_scale=z_plane[:, lo:hi],
+                start=True,
+                stop=True,
+            )
+            nc.scalar.activation(h_neg[t][:, lo:hi], h_banks[t][:, lo:hi], ACT.Copy, scale=-1.0)
+            nc.scalar.copy(h_pos[t][:, lo:hi], h_banks[t][:, lo:hi])
+
+        z_rows = [keep.tile([P, PACK, hi - lo], F32, name="z_rows%d" % lo) for lo, hi in Z_PIECES]
+        z_grouped = [keep.tile([P, PACK * (hi - lo)], BF16, name="z_grouped%d" % lo, align_bytes=64) for lo, hi in Z_PIECES]
+
+        def z_values(c, tiles):
+            lo, hi = Z_PIECES[c]
+            for t in tiles:
+                nc.vector.tensor_tensor(
+                    z_rows[c][:, t, :], s_gained[t][:].indirect(entries(n2_sb, lo, hi)), s_at_n1[:, t, lo:hi], ALU.mult
+                )
+
+        def z_interleave(c, copy):
+            copy(
+                z_grouped[c][:].rearrange("p (a i t) -> p a t i", t=PACK, i=4),
+                z_rows[c][:].rearrange("p t (a i) -> p a t i", i=4),
+            )
+
+        def z_quantize(c):
+            lo, hi = Z_PIECES[c]
+            nc.vector.quantize_mx(out=z_codes[:, lo:hi].bitcast(FP8X4), scales=z_plane[:, lo:hi], in_=z_grouped[c][:])
+            second_product(0, lo, hi)
+
+        z_values(0, range(PACK))
+        z_interleave(0, nc.scalar.copy)
+        z_values(1, range(PACK))
+        z_interleave(1, nc.scalar.copy)
+        quantize_w(0, P)
+        z_values(2, range(0, 2))
+        z_quantize(0)
+        z_values(2, range(2, PACK))
+        z_quantize(1)
+        z_interleave(2, nc.vector.tensor_copy)
+        quantize_w(P, 2 * P)
+        z_quantize(2)
+        quantize_w(2 * P, N)
+        for t in range(1, PACK):
+            second_product(t, 0, S)
+
+        out_rows = out.rearrange("(p t) j -> p t j", t=PACK)
+        above_n4 = [keep.tile([P, S], F32, name="above_n4_%d" % t) for t in range(PACK)]
+        above_n3 = [keep.tile([P, S], F32, name="above_n3_%d" % t) for t in range(PACK)]
+        half_up = [keep.tile([P, S], F32, name="half_up%d" % t) for t in range(PACK)]
+        result = [keep.tile([P, S], F32, name="result%d" % t) for t in range(PACK)]
+
+        def finish(t, lo, hi):
+            nc.vector.scalar_tensor_tensor(
+                result[t][:, lo:hi], above_n3[t][:, lo:hi], 0.0, half_up[t][:, lo:hi], ALU.max, ALU.add
+            )
+            nc.sync.dma_start(out_rows[:, t, lo:hi], result[t][:, lo:hi])
+
+        for t in range(PACK):
+            for lo, hi in HALVES:
+                nc.vector.tensor_tensor(
+                    above_n4[t][:, lo:hi], h_neg[t][:].indirect(entries(n4_sb, lo, hi)), h_pos[t][:, lo:hi], ALU.add
+                )
+                nc.scalar.activation(half_up[t][:, lo:hi], above_n4[t][:, lo:hi], ACT.Relu, scale=-0.5)
+            if t > 0:
+                finish(t - 1, 0, S)
+            pieces = LAST_PIECES if t == PACK - 1 else HALVES
+            for lo, hi in pieces:
+                nc.vector.tensor_tensor(
+                    above_n3[t][:, lo:hi], h_neg[t][:].indirect(entries(n3_sb, lo, hi)), h_pos[t][:, lo:hi], ALU.add
+                )
+        for lo, hi in LAST_PIECES:
+            finish(PACK - 1, lo, hi)

@@ -19,7 +19,7 @@ P = 128
 PACK = 4
 HALVES = [(0, 256), (256, 512)]
 Z_PIECES = [(0, 256), (256, 384), (384, 512)]
-LAST_PIECES = [(0, 256), (256, 384), (384, 512)]
+LAST_PIECES = [(0, 256), (256, 512)]
 
 
 def entries(offsets, lo, hi):
@@ -40,6 +40,9 @@ def tile_picked_keyprodhinge_none_p_kernel(
         d_plane = keep.tile([P, H], U8, align_bytes=64)
         nc.vector.memset(x_scale_table[:].bitcast(I32), 0)
         nc.vector.memset(d_plane[:].bitcast(I32), 0)
+        windows = [keep.tile([P, 2 * S], F32, name="window%d" % t) for t in range(PACK)]
+        for t in range(PACK):
+            nc.vector.memset(windows[t][:, S:], 0.0)
 
         kidx_sb = lists.tile([P, H // 16], U16)
         offs_sb = lists.tile([P, S // 16], U16)
@@ -50,8 +53,8 @@ def tile_picked_keyprodhinge_none_p_kernel(
         d_word_table = keep.tile([P, G], U32, align_bytes=64)
         x_word_table = keep.tile([P, T], U32, align_bytes=64)
         gn_sb = keep.tile([P, PACK], F32)
-        w_raw = keep.tile([P, PACK, N], F32)
 
+        w_raw = keep.tile([P, PACK, N], F32)
         nc.sync.dma_start(kidx_sb[:], kidx)
         nc.sync.dma_start(
             d_scale_table[:].bitcast(I32), d_scales[0].bitcast(I32).unsqueeze(1).broadcast_to([16, 8, G // 4])
@@ -82,8 +85,8 @@ def tile_picked_keyprodhinge_none_p_kernel(
         nc.vector.tensor_copy(d_scale_picked[:], d_scale_table[:].indirect(kidx_sb[:]))
         d_scale_dealt = keep.tile([P, H], U8, align_bytes=64)
         nc.vector.tensor_copy(
-            d_scale_dealt[:].rearrange("p (t m) -> p m t", t=PACK),
-            d_scale_picked[:].rearrange("p (m t) -> p m t", t=PACK),
+            d_scale_dealt[:].rearrange("p (t a i) -> p a t i", t=PACK, i=16),
+            d_scale_picked[:].rearrange("p (a i t) -> p a t i", t=PACK, i=16),
         )
         for q in range(4):
             nc.scalar.dma_start(
@@ -92,61 +95,63 @@ def tile_picked_keyprodhinge_none_p_kernel(
             )
         x_plane = keep.tile([P, S], U8, align_bytes=64)
         nc.vector.tensor_copy(x_plane[:], x_scale_table[:].indirect(offs_sb[:]))
-
         d_word_picked = keep.tile([P, H], U32, align_bytes=64)
         nc.vector.tensor_copy(d_word_picked[:], d_word_table[:].indirect(kidx_sb[:]))
         d_codes = keep.tile([P, H], U32, align_bytes=64)
-        nc.vector.tensor_copy(
-            d_codes[:].rearrange("p (t a i) -> p a t i", t=PACK, i=4),
-            d_word_picked[:].rearrange("p (a i t) -> p a t i", t=PACK, i=4),
-        )
+
+        def deal_words(t0, t1):
+            nc.vector.tensor_copy(
+                d_codes[:].rearrange("p (t a i) -> p a t i", t=PACK, i=4)[:, :, t0:t1, :],
+                d_word_picked[:].rearrange("p (a i t) -> p a t i", t=PACK, i=4)[:, :, t0:t1, :],
+            )
 
         x_codes = keep.tile([P, S], U32, align_bytes=64)
-        s_banks = [psum.tile([P, S], F32, name="s_bank%d" % t) for t in range(PACK)]
+        s_gained = [keep.tile([P, S], F32, name="s_gained%d" % t) for t in range(PACK)]
+
+        def first_product(t, lo, hi, bank):
+            cols = slice(t * P, (t + 1) * P)
+            nc.tensor.matmul_mx(
+                out=bank,
+                lhsT=d_codes[:, cols].bitcast(FP8X4),
+                lhsT_scale=d_plane[:, cols],
+                rhs=x_codes[:, lo:hi].bitcast(FP8X4),
+                rhs_scale=x_plane[:, lo:hi],
+                start=True,
+                stop=True,
+            )
+            nc.scalar.copy(windows[t][:, lo:hi], bank)
+
+        deal_words(0, 1)
         for lo, hi in HALVES:
             nc.vector.tensor_copy(x_codes[:, lo:hi], x_word_table[:].indirect(entries(offs_sb, lo, hi)))
-        for lo, hi in HALVES:
-            for t in range(PACK):
-                cols = slice(t * P, (t + 1) * P)
-                nc.tensor.matmul_mx(
-                    out=s_banks[t][:, lo:hi],
-                    lhsT=d_codes[:, cols].bitcast(FP8X4),
-                    lhsT_scale=d_plane[:, cols],
-                    rhs=x_codes[:, lo:hi].bitcast(FP8X4),
-                    rhs_scale=x_plane[:, lo:hi],
-                    start=True,
-                    stop=True,
-                )
-
-        s_plain = [keep.tile([P, S], F32, name="s_plain%d" % t) for t in range(PACK)]
-        s_gained = [keep.tile([P, S], F32, name="s_gained%d" % t) for t in range(PACK)]
-        for t in range(PACK):
-            nc.scalar.copy(s_plain[t][:], s_banks[t][:])
-        for t in range(PACK):
-            nc.scalar.activation(s_gained[t][:], s_banks[t][:], ACT.Copy, scale=gain[:, t : t + 1])
+        deal_words(1, PACK)
+        s_parts = [(0, lo, hi) for lo, hi in HALVES] + [(t, 0, S) for t in range(1, PACK)]
+        s_banks = [psum.tile([P, hi - lo], F32, name="bank%d" % b) for b, (t, lo, hi) in enumerate(s_parts)]
+        for (t, lo, hi), bank in zip(s_parts, s_banks):
+            first_product(t, lo, hi, bank[:])
+        for (t, lo, hi), bank in zip(s_parts, s_banks):
+            nc.scalar.activation(s_gained[t][:, lo:hi], bank[:], ACT.Copy, scale=gain[:, t : t + 1])
 
         s_at_n1 = keep.tile([P, PACK, S], F32)
         for t in range(PACK):
-            for lo, hi in HALVES:
-                nc.vector.tensor_copy(s_at_n1[:, t, lo:hi], s_plain[t][:].indirect(entries(n1_sb, lo, hi)))
+            nc.vector.tensor_copy(s_at_n1[:, t, :], windows[t][:].indirect(n1_sb[:]))
 
-        w_grouped = keep.tile([P, N * PACK], BF16, align_bytes=64)
-        nc.scalar.copy(
-            w_grouped[:].rearrange("p (t m j) -> p m t j", t=PACK, j=PACK),
-            w_raw[:].rearrange("p j (m t) -> p m t j", t=PACK),
-        )
         w_codes = keep.tile([P, N], U32, align_bytes=64)
         w_plane = keep.tile([P, N], U8, align_bytes=64)
-
-        def quantize_w(lo, hi):
-            nc.vector.quantize_mx(
-                out=w_codes[:, lo:hi].bitcast(FP8X4), scales=w_plane[:, lo:hi], in_=w_grouped[:, PACK * lo : PACK * hi]
+        w_grouped = keep.tile([P, PACK, P * PACK], BF16, tag="x_codes", align_bytes=64)
+        for t in range(PACK):
+            nc.scalar.copy(
+                w_grouped[:, t, :].rearrange("p (a i j) -> p a j i", j=PACK, i=4).rearrange("p (b u) j i -> p b u j i", u=2),
+                w_raw[:].rearrange("p j (b t u i) -> p t b u j i", t=PACK, u=2, i=4)[:, t],
             )
+
+        def quantize_w(t):
+            cols = slice(t * P, (t + 1) * P)
+            nc.vector.quantize_mx(out=w_codes[:, cols].bitcast(FP8X4), scales=w_plane[:, cols], in_=w_grouped[:, t, :])
 
         z_codes = keep.tile([P, S], U32, align_bytes=64)
         z_plane = keep.tile([P, S], U8, align_bytes=64)
-        h_banks = [psum.tile([P, S], F32, name="h_bank%d" % t) for t in range(PACK)]
-        h_neg = [keep.tile([P, S], F32, name="h_neg%d" % t) for t in range(PACK)]
+        h_banks = [psum.tile([P, S], F32, name="h_bank%d" % t, tag="bank%d" % ((t + 5) % 8)) for t in range(PACK)]
         h_pos = [keep.tile([P, S], F32, name="h_pos%d" % t) for t in range(PACK)]
 
         def second_product(t, lo, hi):
@@ -160,7 +165,7 @@ def tile_picked_keyprodhinge_none_p_kernel(
                 start=True,
                 stop=True,
             )
-            nc.scalar.activation(h_neg[t][:, lo:hi], h_banks[t][:, lo:hi], ACT.Copy, scale=-1.0)
+            nc.scalar.activation(windows[t][:, lo:hi], h_banks[t][:, lo:hi], ACT.Copy, scale=-1.0)
             nc.scalar.copy(h_pos[t][:, lo:hi], h_banks[t][:, lo:hi])
 
         z_rows = [keep.tile([P, PACK, hi - lo], F32, name="z_rows%d" % lo) for lo, hi in Z_PIECES]
@@ -188,19 +193,20 @@ def tile_picked_keyprodhinge_none_p_kernel(
         z_interleave(0, nc.scalar.copy)
         z_values(1, range(PACK))
         z_interleave(1, nc.scalar.copy)
-        quantize_w(0, P)
+        quantize_w(0)
         z_values(2, range(0, 2))
         z_quantize(0)
         z_values(2, range(2, PACK))
         z_quantize(1)
         z_interleave(2, nc.vector.tensor_copy)
-        quantize_w(P, 2 * P)
+        quantize_w(1)
         z_quantize(2)
-        quantize_w(2 * P, N)
+        quantize_w(2)
+        quantize_w(3)
         for t in range(1, PACK):
             second_product(t, 0, S)
 
-        out_rows = out.rearrange("(p t) j -> p t j", t=PACK)
+        out_rows = out.rearrange("(b t q) j -> t b q j", t=PACK, q=8)
         above_n4 = [keep.tile([P, S], F32, name="above_n4_%d" % t) for t in range(PACK)]
         above_n3 = [keep.tile([P, S], F32, name="above_n3_%d" % t) for t in range(PACK)]
         half_up = [keep.tile([P, S], F32, name="half_up%d" % t) for t in range(PACK)]
@@ -210,20 +216,17 @@ def tile_picked_keyprodhinge_none_p_kernel(
             nc.vector.scalar_tensor_tensor(
                 result[t][:, lo:hi], above_n3[t][:, lo:hi], 0.0, half_up[t][:, lo:hi], ALU.max, ALU.add
             )
-            nc.sync.dma_start(out_rows[:, t, lo:hi], result[t][:, lo:hi])
+            nc.sync.dma_start(out_rows[t][:, :, lo:hi], result[t][:, lo:hi])
 
         for t in range(PACK):
-            for lo, hi in HALVES:
-                nc.vector.tensor_tensor(
-                    above_n4[t][:, lo:hi], h_neg[t][:].indirect(entries(n4_sb, lo, hi)), h_pos[t][:, lo:hi], ALU.add
-                )
-                nc.scalar.activation(half_up[t][:, lo:hi], above_n4[t][:, lo:hi], ACT.Relu, scale=-0.5)
+            nc.vector.tensor_tensor(above_n4[t][:], windows[t][:].indirect(n4_sb[:]), h_pos[t][:], ALU.add)
+            nc.scalar.activation(half_up[t][:], above_n4[t][:], ACT.Relu, scale=-0.5)
             if t > 0:
                 finish(t - 1, 0, S)
-            pieces = LAST_PIECES if t == PACK - 1 else HALVES
+            pieces = LAST_PIECES if t == PACK - 1 else [(0, S)]
             for lo, hi in pieces:
                 nc.vector.tensor_tensor(
-                    above_n3[t][:, lo:hi], h_neg[t][:].indirect(entries(n3_sb, lo, hi)), h_pos[t][:, lo:hi], ALU.add
+                    above_n3[t][:, lo:hi], windows[t][:].indirect(entries(n3_sb, lo, hi)), h_pos[t][:, lo:hi], ALU.add
                 )
         for lo, hi in LAST_PIECES:
             finish(PACK - 1, lo, hi)

@@ -40,9 +40,10 @@ def tile_picked_keyprodhinge_none_p_kernel(
         d_plane = keep.tile([P, H], U8, align_bytes=64)
         nc.vector.memset(x_scale_table[:].bitcast(I32), 0)
         nc.vector.memset(d_plane[:].bitcast(I32), 0)
-        windows = [keep.tile([P, 2 * S], F32, name="window%d" % t) for t in range(PACK)]
-        for t in range(PACK):
-            nc.vector.memset(windows[t][:, S:], 0.0)
+        windows = [keep.tile([P, 2 * S], F32, name="window%d" % t) for t in range(PACK + 1)]
+        for window in windows:
+            nc.vector.memset(window[:, S:], 0.0)
+        h_windows = [windows[PACK]] + windows[1:PACK]
 
         kidx_sb = lists.tile([P, H // 16], U16)
         offs_sb = lists.tile([P, S // 16], U16)
@@ -78,8 +79,9 @@ def tile_picked_keyprodhinge_none_p_kernel(
         nc.sync.dma_start(n3_sb[:], n3)
         nc.sync.dma_start(n4_sb[:], n4)
 
-        gain = keep.tile([P, PACK], F32)
-        nc.scalar.activation(gain[:], gn_sb[:], ACT.Copy, scale=0.0625 * 0.0625)
+        gain = keep.tile([P, PACK, S], F32)
+        for t in range(PACK):
+            nc.scalar.copy(gain[:, t, :], gn_sb[:, t : t + 1].to_broadcast([P, S]))
 
         d_scale_picked = keep.tile([P, H], U8, align_bytes=64)
         nc.vector.tensor_copy(d_scale_picked[:], d_scale_table[:].indirect(kidx_sb[:]))
@@ -106,7 +108,6 @@ def tile_picked_keyprodhinge_none_p_kernel(
             )
 
         x_codes = keep.tile([P, S], U32, align_bytes=64)
-        s_gained = [keep.tile([P, S], F32, name="s_gained%d" % t) for t in range(PACK)]
 
         def first_product(t, lo, hi, bank):
             cols = slice(t * P, (t + 1) * P)
@@ -119,7 +120,7 @@ def tile_picked_keyprodhinge_none_p_kernel(
                 start=True,
                 stop=True,
             )
-            nc.scalar.copy(windows[t][:, lo:hi], bank)
+            nc.scalar.activation(windows[t][:, lo:hi], bank, ACT.Copy, scale=0.0625)
 
         deal_words(0, 1)
         for lo, hi in HALVES:
@@ -129,12 +130,10 @@ def tile_picked_keyprodhinge_none_p_kernel(
         s_banks = [psum.tile([P, hi - lo], F32, name="bank%d" % b) for b, (t, lo, hi) in enumerate(s_parts)]
         for (t, lo, hi), bank in zip(s_parts, s_banks):
             first_product(t, lo, hi, bank[:])
-        for (t, lo, hi), bank in zip(s_parts, s_banks):
-            nc.scalar.activation(s_gained[t][:, lo:hi], bank[:], ACT.Copy, scale=gain[:, t : t + 1])
 
         s_at_n1 = keep.tile([P, PACK, S], F32)
         for t in range(PACK):
-            nc.vector.tensor_copy(s_at_n1[:, t, :], windows[t][:].indirect(n1_sb[:]))
+            nc.vector.tensor_tensor(s_at_n1[:, t, :], windows[t][:].indirect(n1_sb[:]), gain[:, t, :], ALU.mult)
 
         w_codes = keep.tile([P, N], U32, align_bytes=64)
         w_plane = keep.tile([P, N], U8, align_bytes=64)
@@ -151,13 +150,13 @@ def tile_picked_keyprodhinge_none_p_kernel(
 
         z_codes = keep.tile([P, S], U32, align_bytes=64)
         z_plane = keep.tile([P, S], U8, align_bytes=64)
-        h_banks = [psum.tile([P, S], F32, name="h_bank%d" % t, tag="bank%d" % ((t + 5) % 8)) for t in range(PACK)]
         h_pos = [keep.tile([P, S], F32, name="h_pos%d" % t) for t in range(PACK)]
 
-        def second_product(t, lo, hi):
+        def second_product(t, lo, hi, tag):
             cols = slice(t * P, (t + 1) * P)
+            bank = psum.tile([P, hi - lo], F32, name="h_bank", tag=tag)
             nc.tensor.matmul_mx(
-                out=h_banks[t][:, lo:hi],
+                out=bank[:],
                 lhsT=w_codes[:, cols].bitcast(FP8X4),
                 lhsT_scale=w_plane[:, cols],
                 rhs=z_codes[:, lo:hi].bitcast(FP8X4),
@@ -165,46 +164,44 @@ def tile_picked_keyprodhinge_none_p_kernel(
                 start=True,
                 stop=True,
             )
-            nc.scalar.activation(windows[t][:, lo:hi], h_banks[t][:, lo:hi], ACT.Copy, scale=-1.0)
-            nc.scalar.copy(h_pos[t][:, lo:hi], h_banks[t][:, lo:hi])
+            nc.scalar.activation(h_windows[t][:, lo:hi], bank[:], ACT.Copy, scale=-1.0)
+            nc.scalar.copy(h_pos[t][:, lo:hi], bank[:])
 
-        z_rows = [keep.tile([P, PACK, hi - lo], F32, name="z_rows%d" % lo) for lo, hi in Z_PIECES]
-        z_grouped = [keep.tile([P, PACK * (hi - lo)], BF16, name="z_grouped%d" % lo, align_bytes=64) for lo, hi in Z_PIECES]
-
-        def z_values(c, tiles):
+        def z_values(c, tag):
             lo, hi = Z_PIECES[c]
-            for t in tiles:
+            rows = keep.tile([P, PACK, hi - lo], F32, name="z_rows", tag=tag, align_bytes=64)
+            for t in range(PACK):
                 nc.vector.tensor_tensor(
-                    z_rows[c][:, t, :], s_gained[t][:].indirect(entries(n2_sb, lo, hi)), s_at_n1[:, t, lo:hi], ALU.mult
+                    rows[:, t, :], windows[t][:].indirect(entries(n2_sb, lo, hi)), s_at_n1[:, t, lo:hi], ALU.mult
                 )
+            return rows
 
-        def z_interleave(c, copy):
+        def z_interleave(rows, copy, tag):
+            grouped = keep.tile([P, PACK * rows.shape[2]], BF16, name="z_grouped", tag=tag, align_bytes=64)
             copy(
-                z_grouped[c][:].rearrange("p (a i t) -> p a t i", t=PACK, i=4),
-                z_rows[c][:].rearrange("p t (a i) -> p a t i", i=4),
+                grouped[:].rearrange("p (a i t) -> p a t i", t=PACK, i=4),
+                rows[:].rearrange("p t (a i) -> p a t i", i=4),
             )
+            return grouped
 
-        def z_quantize(c):
+        def z_quantize(c, grouped):
             lo, hi = Z_PIECES[c]
-            nc.vector.quantize_mx(out=z_codes[:, lo:hi].bitcast(FP8X4), scales=z_plane[:, lo:hi], in_=z_grouped[c][:])
-            second_product(0, lo, hi)
+            nc.vector.quantize_mx(out=z_codes[:, lo:hi].bitcast(FP8X4), scales=z_plane[:, lo:hi], in_=grouped[:])
+            second_product(0, lo, hi, "bank%d" % (5 + c))
 
-        z_values(0, range(PACK))
-        z_interleave(0, nc.scalar.copy)
-        z_values(1, range(PACK))
-        z_interleave(1, nc.scalar.copy)
+        grouped0 = z_interleave(z_values(0, "z_rows0"), nc.scalar.copy, "z_grouped0")
+        grouped1 = z_interleave(z_values(1, "z_rows1"), nc.scalar.copy, "z_grouped1")
         quantize_w(0)
-        z_values(2, range(0, 2))
-        z_quantize(0)
-        z_values(2, range(2, PACK))
-        z_quantize(1)
-        z_interleave(2, nc.vector.tensor_copy)
+        z_quantize(0, grouped0)
+        rows2 = z_values(2, "z_grouped0")
+        z_quantize(1, grouped1)
+        grouped2 = z_interleave(rows2, nc.vector.tensor_copy, "z_grouped2")
         quantize_w(1)
-        z_quantize(2)
+        z_quantize(2, grouped2)
         quantize_w(2)
         quantize_w(3)
         for t in range(1, PACK):
-            second_product(t, 0, S)
+            second_product(t, 0, S, "bank%d" % (t - 1))
 
         out_rows = out.rearrange("(b t q) j -> t b q j", t=PACK, q=8)
         above_n4 = [keep.tile([P, S], F32, name="above_n4_%d" % t) for t in range(PACK)]
@@ -219,14 +216,17 @@ def tile_picked_keyprodhinge_none_p_kernel(
             nc.sync.dma_start(out_rows[t][:, :, lo:hi], result[t][:, lo:hi])
 
         for t in range(PACK):
-            nc.vector.tensor_tensor(above_n4[t][:], windows[t][:].indirect(n4_sb[:]), h_pos[t][:], ALU.add)
+            for lo, hi in HALVES if t == 0 else [(0, S)]:
+                nc.vector.tensor_tensor(
+                    above_n4[t][:, lo:hi], h_windows[t][:].indirect(entries(n4_sb, lo, hi)), h_pos[t][:, lo:hi], ALU.add
+                )
             nc.scalar.activation(half_up[t][:], above_n4[t][:], ACT.Relu, scale=-0.5)
             if t > 0:
                 finish(t - 1, 0, S)
             pieces = LAST_PIECES if t == PACK - 1 else [(0, S)]
             for lo, hi in pieces:
                 nc.vector.tensor_tensor(
-                    above_n3[t][:, lo:hi], windows[t][:].indirect(entries(n3_sb, lo, hi)), h_pos[t][:, lo:hi], ALU.add
+                    above_n3[t][:, lo:hi], h_windows[t][:].indirect(entries(n3_sb, lo, hi)), h_pos[t][:, lo:hi], ALU.add
                 )
         for lo, hi in LAST_PIECES:
             finish(PACK - 1, lo, hi)

from contextlib import ExitStack

import concourse.mybir as mybir

K, T, S, N, G, H = 512, 2048, 512, 512, 2048, 512
FLOPS = 2 * K * H * S + 2 * H * N * S

F32 = mybir.dt.float32
BF16 = mybir.dt.bfloat16
I32 = mybir.dt.int32
U32 = mybir.dt.uint32
U16 = mybir.dt.uint16
U8 = mybir.dt.uint8
FP8X4 = mybir.dt.float8_e4m3fn_x4
ALU = mybir.AluOpType
ACT = mybir.ActivationFunctionType

P = 128
PACK = 4
HALVES = [(0, 256), (256, 512)]
Z_PIECES = [(0, 256), (256, 384), (384, 512)]
LAST_PIECES = [(0, 256), (256, 512)]


def entries(offsets, lo, hi):
    return offsets[:, lo // 16 : hi // 16]


def tile_picked_keyprodhinge_none_p_kernel(
    tc, x_words, x_scales, d_words, d_scales, gn, w1, offs, kidx, n1, n2, n3, n4, out
):
    nc = tc.nc
    with ExitStack() as ctx:
        lists = ctx.enter_context(tc.tile_pool(name="lists", bufs=1))
        keep = ctx.enter_context(tc.tile_pool(name="keep", bufs=1))
        psum = ctx.enter_context(tc.psum_pool(name="psum", bufs=1))

        d_scale_table = keep.tile([P, G], U8, align_bytes=64)
        x_scale_table = keep.tile([P, T], U8, align_bytes=64)
        d_plane = keep.tile([P, H], U8, align_bytes=64)
        nc.vector.memset(x_scale_table[:].bitcast(I32), 0)
        nc.vector.memset(d_plane[:].bitcast(I32), 0)
        windows = [keep.tile([P, 2 * S], F32, name="window%d" % t) for t in range(PACK + 1)]
        for window in windows:
            nc.vector.memset(window[:, S:], 0.0)
        h_windows = [windows[PACK]] + windows[1:PACK]

        kidx_sb = lists.tile([P, H // 16], U16)
        offs_sb = lists.tile([P, S // 16], U16)
        n1_sb = lists.tile([P, S // 16], U16)
        n2_sb = lists.tile([P, S // 16], U16)
        n3_sb = lists.tile([P, S // 16], U16)
        n4_sb = lists.tile([P, S // 16], U16)
        d_word_table = keep.tile([P, G], U32, align_bytes=64)
        x_word_table = keep.tile([P, T], U32, align_bytes=64)
        gn_sb = keep.tile([P, PACK], F32)

        w_raw = keep.tile([P, PACK, N], F32)
        nc.sync.dma_start(kidx_sb[:], kidx)
        nc.sync.dma_start(
            d_scale_table[:].bitcast(I32), d_scales[0].bitcast(I32).unsqueeze(1).broadcast_to([16, 8, G // 4])
        )
        for q in range(4):
            nc.scalar.dma_start(
                x_scale_table[:].bitcast(I32)[32 * q : 32 * q + 4, :],
                x_scales[0].bitcast(I32)[4 * q : 4 * q + 4, :],
            )
        nc.sync.dma_start(offs_sb[:], offs)
        nc.sync.dma_start(
            d_word_table[:].bitcast(I32), d_words[0].rearrange("p n t -> p (n t)").bitcast(I32)
        )
        nc.sync.dma_start(gn_sb[:], gn.rearrange("(p t) o -> p (t o)", t=PACK))
        nc.sync.dma_start(
            x_word_table[:].bitcast(I32), x_words[0].rearrange("p n t -> p (n t)").bitcast(I32)
        )
        nc.sync.dma_start(n1_sb[:], n1)
        nc.sync.dma_start(n2_sb[:], n2)
        nc.sync.dma_start(w_raw[:], w1.rearrange("(p j) n -> p j n", j=PACK))
        nc.sync.dma_start(n3_sb[:], n3)
        nc.sync.dma_start(n4_sb[:], n4)

        gain = keep.tile([P, PACK, S], F32)
        for t in range(PACK):
            nc.scalar.copy(gain[:, t, :], gn_sb[:, t : t + 1].to_broadcast([P, S]))

        d_scale_picked = keep.tile([P, H], U8, align_bytes=64)
        nc.vector.tensor_copy(d_scale_picked[:], d_scale_table[:].indirect(kidx_sb[:]))
        d_scale_dealt = keep.tile([P, H], U8, align_bytes=64)
        nc.vector.tensor_copy(
            d_scale_dealt[:].rearrange("p (t a i) -> p a t i", t=PACK, i=16),
            d_scale_picked[:].rearrange("p (a i t) -> p a t i", t=PACK, i=16),
        )
        for q in range(4):
            nc.scalar.dma_start(
                d_plane[:].bitcast(I32)[32 * q : 32 * q + 4, :],
                d_scale_dealt[:].bitcast(I32)[32 * q : 32 * q + 32 : 8, :],
            )
        x_plane = keep.tile([P, S], U8, align_bytes=64)
        nc.vector.tensor_copy(x_plane[:], x_scale_table[:].indirect(offs_sb[:]))
        d_word_picked = keep.tile([P, H], U32, align_bytes=64)
        nc.vector.tensor_copy(d_word_picked[:], d_word_table[:].indirect(kidx_sb[:]))
        d_codes = keep.tile([P, H], U32, align_bytes=64)

        def deal_words(t0, t1):
            nc.vector.tensor_copy(
                d_codes[:].rearrange("p (t a i) -> p a t i", t=PACK, i=4)[:, :, t0:t1, :],
                d_word_picked[:].rearrange("p (a i t) -> p a t i", t=PACK, i=4)[:, :, t0:t1, :],
            )

        x_codes = keep.tile([P, S], U32, align_bytes=64)

        def first_product(t, lo, hi, bank):
            cols = slice(t * P, (t + 1) * P)
            nc.tensor.matmul_mx(
                out=bank,
                lhsT=d_codes[:, cols].bitcast(FP8X4),
                lhsT_scale=d_plane[:, cols],
                rhs=x_codes[:, lo:hi].bitcast(FP8X4),
                rhs_scale=x_plane[:, lo:hi],
                start=True,
                stop=True,
            )
            nc.scalar.activation(windows[t][:, lo:hi], bank, ACT.Copy, scale=0.0625)

        deal_words(0, 1)
        for lo, hi in HALVES:
            nc.vector.tensor_copy(x_codes[:, lo:hi], x_word_table[:].indirect(entries(offs_sb, lo, hi)))
        deal_words(1, PACK)
        s_parts = [(0, lo, hi) for lo, hi in HALVES] + [(t, 0, S) for t in range(1, PACK)]
        s_banks = [psum.tile([P, hi - lo], F32, name="bank%d" % b) for b, (t, lo, hi) in enumerate(s_parts)]
        for (t, lo, hi), bank in zip(s_parts, s_banks):
            first_product(t, lo, hi, bank[:])

        s_at_n1 = keep.tile([P, PACK, S], F32)
        for t in range(PACK):
            nc.vector.tensor_tensor(s_at_n1[:, t, :], windows[t][:].indirect(n1_sb[:]), gain[:, t, :], ALU.mult)

        w_codes = keep.tile([P, N], U32, align_bytes=64)
        w_plane = keep.tile([P, N], U8, align_bytes=64)
        w_grouped = keep.tile([P, PACK, P * PACK], BF16, tag="x_codes", align_bytes=64)
        for t in range(PACK):
            nc.scalar.copy(
                w_grouped[:, t, :].rearrange("p (a i j) -> p a j i", j=PACK, i=4).rearrange("p (b u) j i -> p b u j i", u=2),
                w_raw[:].rearrange("p j (b t u i) -> p t b u j i", t=PACK, u=2, i=4)[:, t],
            )

        def quantize_w(t):
            cols = slice(t * P, (t + 1) * P)
            nc.vector.quantize_mx(out=w_codes[:, cols].bitcast(FP8X4), scales=w_plane[:, cols], in_=w_grouped[:, t, :])

        z_codes = keep.tile([P, S], U32, align_bytes=64)
        z_plane = keep.tile([P, S], U8, align_bytes=64)
        h_pos = [keep.tile([P, S], F32, name="h_pos%d" % t) for t in range(PACK)]

        def second_product(t, lo, hi, tag):
            cols = slice(t * P, (t + 1) * P)
            bank = psum.tile([P, hi - lo], F32, name="h_bank", tag=tag)
            nc.tensor.matmul_mx(
                out=bank[:],
                lhsT=w_codes[:, cols].bitcast(FP8X4),
                lhsT_scale=w_plane[:, cols],
                rhs=z_codes[:, lo:hi].bitcast(FP8X4),
                rhs_scale=z_plane[:, lo:hi],
                start=True,
                stop=True,
            )
            nc.scalar.activation(h_windows[t][:, lo:hi], bank[:], ACT.Copy, scale=-1.0)
            nc.scalar.copy(h_pos[t][:, lo:hi], bank[:])

        def z_values(c, tag):
            lo, hi = Z_PIECES[c]
            rows = keep.tile([P, PACK, hi - lo], F32, name="z_rows", tag=tag, align_bytes=64)
            for t in range(PACK):
                nc.vector.tensor_tensor(
                    rows[:, t, :], windows[t][:].indirect(entries(n2_sb, lo, hi)), s_at_n1[:, t, lo:hi], ALU.mult
                )
            return rows

        def z_interleave(rows, copy, tag):
            grouped = keep.tile([P, PACK * rows.shape[2]], BF16, name="z_grouped", tag=tag, align_bytes=64)
            copy(
                grouped[:].rearrange("p (a i t) -> p a t i", t=PACK, i=4),
                rows[:].rearrange("p t (a i) -> p a t i", i=4),
            )
            return grouped

        def z_quantize(c, grouped):
            lo, hi = Z_PIECES[c]
            nc.vector.quantize_mx(out=z_codes[:, lo:hi].bitcast(FP8X4), scales=z_plane[:, lo:hi], in_=grouped[:])
            second_product(0, lo, hi, "bank%d" % (5 + c))

        grouped0 = z_interleave(z_values(0, "z_rows0"), nc.scalar.copy, "z_grouped0")
        grouped1 = z_interleave(z_values(1, "z_rows1"), nc.scalar.copy, "z_grouped1")
        quantize_w(0)
        z_quantize(0, grouped0)
        rows2 = z_values(2, "z_grouped0")
        z_quantize(1, grouped1)
        grouped2 = z_interleave(rows2, nc.vector.tensor_copy, "z_grouped2")
        quantize_w(1)
        z_quantize(2, grouped2)
        quantize_w(2)
        quantize_w(3)
        for t in range(1, PACK):
            second_product(t, 0, S, "bank%d" % (t - 1))

        out_rows = out.rearrange("(b t q) j -> t b q j", t=PACK, q=8)
        above_n4 = [keep.tile([P, S], F32, name="above_n4_%d" % t) for t in range(PACK)]
        above_n3 = [keep.tile([P, S], F32, name="above_n3_%d" % t) for t in range(PACK)]
        half_up = [keep.tile([P, S], F32, name="half_up%d" % t) for t in range(PACK)]
        result = [keep.tile([P, S], F32, name="result%d" % t) for t in range(PACK)]

        def finish(t, lo, hi):
            nc.vector.scalar_tensor_tensor(
                result[t][:, lo:hi], above_n3[t][:, lo:hi], 0.0, half_up[t][:, lo:hi], ALU.max, ALU.add
            )
            nc.sync.dma_start(out_rows[t][:, :, lo:hi], result[t][:, lo:hi])

        for t in range(PACK):
            for lo, hi in HALVES if t == 0 else [(0, S)]:
                nc.vector.tensor_tensor(
                    above_n4[t][:, lo:hi], h_windows[t][:].indirect(entries(n4_sb, lo, hi)), h_pos[t][:, lo:hi], ALU.add
                )
            nc.scalar.activation(half_up[t][:], above_n4[t][:], ACT.Relu, scale=-0.5)
            if t > 0:
                finish(t - 1, 0, S)
            pieces = LAST_PIECES if t == PACK - 1 else [(0, S)]
            for lo, hi in pieces:
                nc.vector.tensor_tensor(
                    above_n3[t][:, lo:hi], h_windows[t][:].indirect(entries(n3_sb, lo, hi)), h_pos[t][:, lo:hi], ALU.add
                )
        for lo, hi in LAST_PIECES:
            finish(PACK - 1, lo, hi)
